import numpy as np
import ml_dtypes


def mxq(x, axis, fmt="e4m3"):
    dtype, down = {"e4m3": (ml_dtypes.float8_e4m3fn, 7), "e5m2": (ml_dtypes.float8_e5m2, 14)}[fmt]
    v = np.moveaxis(np.asarray(x, np.float32).astype(ml_dtypes.bfloat16).astype(np.float64), axis, -1)
    blocks = v.reshape(v.shape[:-1] + (-1, 32))
    amax = np.abs(blocks).max(-1, keepdims=True)
    byte = np.maximum(np.where(amax > 0, np.frexp(amax)[1] - 1 + 127, 0) - down, 1)
    scale = np.exp2(byte - 127.0)
    codes = (blocks / scale).astype(np.float32).astype(dtype).astype(np.float64)
    return np.moveaxis((codes * scale).reshape(v.shape), -1, axis)


WIDE = False


def mx_kscale(k):
    if not WIDE:
        return np.ones(k)
    levels = np.array([10, -10, 5, -5, 0])
    if k % 512:
        return np.exp2(np.random.permutation(np.resize(levels, k // 32))).repeat(32)
    a = np.empty((k // 512, 16))
    for p in range(k // 512):
        a[p, :8] = np.random.permutation(np.resize(levels, 8))
        for g in range(8):
            far = levels[np.abs(levels - a[p, g]) >= 10]
            a[p, g + 8] = far[np.random.randint(len(far))]
    return np.exp2(a.ravel()).repeat(32)


def f64(x):
    return np.asarray(x).astype(np.float64)


def striped(idx):
    return np.tile(np.asarray(idx).reshape(-1, 16).T, (8, 1)).astype(np.uint16)


def unstriped(offs):
    return offs[:16].T.reshape(-1).astype(np.int64)


def striped8(idx):
    return np.asarray(idx).reshape(8, -1, 16).transpose(0, 2, 1).reshape(128, -1).astype(np.uint16)


def unstriped8(offs):
    return offs.reshape(8, 16, -1).transpose(0, 2, 1).reshape(8, -1).astype(np.int64)


def pick8(x, idx, run):
    r = np.arange(len(x))
    return x[r[:, None], idx[r % (8 * run) // run]]


E2M1 = np.array([0.0, 0.5, 1.0, 1.5, 2.0, 3.0, 4.0, 6.0, -0.0, -0.5, -1.0, -1.5, -2.0, -3.0, -4.0, -6.0])


def pack_weight(w, fmt):
    k, n = w.shape
    w = f64(np.asarray(w, np.float32).astype(ml_dtypes.bfloat16)).reshape(k // 32, 32, n)
    amax = np.abs(w).max(1)
    if fmt == "e4m3":
        byte = np.frexp(amax)[1] - 1 + 127 - 7
    else:
        mant, ex = np.frexp(amax / 6.0)
        byte = np.where(mant > 0.5, ex, ex - 1) + 127
    byte = np.clip(np.where(amax > 0, byte, 1), 1, 254)
    scaled = (w * np.exp2(127.0 - byte)[:, None, :]).reshape(k, n).astype(np.float32)
    by_word = np.ascontiguousarray(scaled.reshape(k // 512, 128, 4, n).transpose(0, 1, 3, 2))
    if fmt == "e4m3":
        words = by_word.astype(ml_dtypes.float8_e4m3fn).view(np.uint8)
    else:
        c = by_word.astype(ml_dtypes.float4_e2m1fn).view(np.uint8) & 0xF
        words = (c[..., 0::2] | (c[..., 1::2] << 4)).reshape(k // 512, 128, 2 * n)
    return np.ascontiguousarray(words), np.ascontiguousarray(byte.astype(np.uint8).reshape(k // 512, 16, n))


def unpack_weight(words, scales, fmt):
    g, _, n = scales.shape
    words = np.ascontiguousarray(words).reshape(g, 128, n, -1)
    if fmt == "e4m3":
        vals = words.view(ml_dtypes.float8_e4m3fn).astype(np.float64)
    else:
        nib = np.empty((g, 128, n, 4), np.uint8)
        nib[..., 0::2] = words & 0xF
        nib[..., 1::2] = words >> 4
        vals = E2M1[nib]
    vals = vals * np.repeat(np.exp2(scales.astype(np.float64) - 127.0), 8, axis=1)[..., None]
    return vals.transpose(0, 1, 3, 2).reshape(g * 512, n)


K, T, J, L, S, N = 512, 1024, 512, 512, 1024, 512


def setup_inputs():
    n = np.random.standard_normal
    idx = np.stack([np.random.permutation(T)[:J] for _ in range(8)])
    idx2 = np.random.permutation(S)[:J]
    fk = mx_kscale(K)
    fl = mx_kscale(L)
    xtp = pack_weight(n((K, T)) / fk[:, None], "e4m3")
    xbp = pack_weight(n((L, S)) / fl[:, None], "e2m1")
    wbp = pack_weight(n((L, N)) * 1 / np.sqrt(L) * fl[:, None], "e4m3")
    return {
        "xt_words": xtp[0],
        "xt_scales": xtp[1],
        "wa": (n((K, N)) * 1 / np.sqrt(K) * fk[:, None]).astype(np.float32),
        "xb_words": xbp[0],
        "xb_scales": xbp[1],
        "wb_words": wbp[0],
        "wb_scales": wbp[1],
        "offs": striped8(idx),
        "offs2": striped(idx2),
    }


def reference(xt_words, xt_scales, wa, xb_words, xb_scales, wb_words, wb_scales, offs, offs2):
    idx = unstriped8(offs)
    idx2 = unstriped(offs2)
    xtu = unpack_weight(xt_words, xt_scales, "e4m3")
    xbu = unpack_weight(xb_words, xb_scales, "e2m1")
    wbu = unpack_weight(wb_words, wb_scales, "e4m3")
    waq = mxq(f64(wa), 0, "e4m3")
    xtidxg = pick8(xtu, idx, 64)
    p = waq.T @ xtidxg
    xbidx2g = xbu[:, idx2]
    q = wbu.T @ xbidx2g
    y = np.maximum(p - 0.7 * q, 0.0)
    return y

@@ -1,0 +1,145 @@
+from contextlib import ExitStack
+
+import concourse.mybir as mybir
+
+F32 = mybir.dt.float32
+BF16 = mybir.dt.bfloat16
+I32 = mybir.dt.int32
+U32 = mybir.dt.uint32
+U16 = mybir.dt.uint16
+U8 = mybir.dt.uint8
+FP8X4 = mybir.dt.float8_e4m3fn_x4
+FP4X4 = mybir.dt.float4_e2m1fn_x4
+ALU = mybir.AluOpType
+ACT = mybir.ActivationFunctionType
+
+P = 128
+T = 1024
+J = 512
+N = 512
+HALF = N // 2
+FLOPS = 2 * 2 * 512 * N * J
+
+
+def tile_moe_expert_heads_against_shared_kernel(
+    tc, xt_words, xt_scales, wa, xb_words, xb_scales, wb_words, wb_scales, offs, offs2, out
+):
+    nc = tc.nc
+    with ExitStack() as ctx:
+        lists = ctx.enter_context(tc.tile_pool(name="lists", bufs=1))
+        sb = ctx.enter_context(tc.tile_pool(name="sb", bufs=1))
+        psum = ctx.enter_context(tc.psum_pool(name="psum", bufs=1))
+
+        xt_list = lists.tile([P, J // 16], U16, name="xt_list")
+        xb_list = lists.tile([P, J // 16], U16, name="xb_list")
+
+        xt_scale_table = sb.tile([P, T], U8, name="xt_scale_table", align_bytes=64)
+        xb_scale_table = sb.tile([P, T], U8, name="xb_scale_table", align_bytes=64)
+        wb_plane = sb.tile([P, N], U8, name="wb_plane", align_bytes=64)
+        xt_plane = sb.tile([P, J], U8, name="xt_plane", align_bytes=64)
+        nc.vector.memset(xt_plane[:].bitcast(I32), 0)
+
+        xt_table = sb.tile([P, T], U32, name="xt_table", align_bytes=64)
+        xb_table = sb.tile([P, T], U16, name="xb_table", tag="reused", align_bytes=64)
+        wb_codes = sb.tile([P, N], U32, name="wb_codes", align_bytes=64)
+        wa_raw = [sb.tile([P, 4, HALF], F32, name="wa_raw%d" % h, align_bytes=64) for h in range(2)]
+        wa_rows = wa.rearrange("(p t) n -> p t n", t=4)
+
+        def load_rows(plane, scales):
+            for x in range(4):
+                rows = scales[0, 4 * x : 4 * x + 4, :].bitcast(I32)
+                nc.sync.dma_start(
+                    plane[32 * x : 32 * x + 32, :].bitcast(I32), rows.unsqueeze(0).to_broadcast([8, 4, rows.shape[1]])
+                )
+
+        nc.sync.dma_start(xt_list[:], offs)
+        nc.sync.dma_start(
+            xt_scale_table[:].bitcast(I32), xt_scales[0].bitcast(I32).unsqueeze(1).to_broadcast([16, 8, T // 4])
+        )
+        nc.sync.dma_start(wa_raw[0][:], wa_rows[:, :, 0:HALF])
+        nc.sync.dma_start(xb_list[:], offs2)
+        load_rows(xb_scale_table, xb_scales)
+        nc.sync.dma_start(xb_table[:].bitcast(I32), xb_words[0].bitcast(I32))
+        nc.sync.dma_start(wa_raw[1][:], wa_rows[:, :, HALF:N])
+        load_rows(wb_plane, wb_scales)
+        nc.sync.dma_start(wb_codes[:].bitcast(I32), wb_words[0].rearrange("p n t -> p (n t)").bitcast(I32))
+        nc.sync.dma_start(xt_table[:].bitcast(I32), xt_words[0].rearrange("p n t -> p (n t)").bitcast(I32))
+
+        xb_plane = sb.tile([P, J], U8, name="xb_plane", align_bytes=64)
+        xb_codes = sb.tile([P, J], U16, name="xb_codes", align_bytes=64)
+        xt_picked = sb.tile([P, J], U8, name="xt_picked", align_bytes=64)
+        nc.vector.tensor_copy(xt_picked[:], xt_scale_table[:].indirect(xt_list[:]))
+        nc.vector.tensor_copy(xb_plane[:], xb_scale_table[:].indirect(xb_list[:]))
+        nc.vector.tensor_copy(xb_codes[:], xb_table[:].indirect(xb_list[:]))
+        for x in range(4):
+            nc.sync.dma_start(
+                xt_plane[32 * x : 32 * x + 4, :].bitcast(I32), xt_picked[32 * x : 32 * x + 32 : 8, :].bitcast(I32)
+            )
+
+        wa_grouped = []
+        for h in range(2):
+            grouped = sb.tile([P, HALF, 4], BF16, name="wa_grouped%d" % h, align_bytes=64)
+            nc.scalar.copy(
+                grouped[:].rearrange("p (c i) t -> p c t i", i=4), wa_raw[h][:].rearrange("p t (c i) -> p c t i", i=4)
+            )
+            wa_grouped.append(grouped)
+
+        q_scaled = sb.tile([P, 4, J], F32, name="q_scaled")
+        for b in range(4):
+            q_bank = psum.tile([P, J], F32, name="q_bank%d" % b)
+            nc.tensor.matmul_mx(
+                out=q_bank[:],
+                lhsT=wb_codes[:, b * P : (b + 1) * P].bitcast(FP8X4),
+                lhsT_scale=wb_plane[:, b * P : (b + 1) * P],
+                rhs=xb_codes[:].bitcast(FP4X4),
+                rhs_scale=xb_plane[:],
+                start=True,
+                stop=True,
+            )
+            nc.scalar.activation(q_scaled[:, b, :], q_bank[:], ACT.Copy, scale=-0.7)
+
+        wa_codes = [
+            sb.tile([P, HALF], U32, name="wa_codes0", tag="reused", align_bytes=64),
+            sb.tile([P, HALF], U32, name="wa_codes1", align_bytes=64),
+        ]
+        wa_plane = [sb.tile([P, HALF], U8, name="wa_plane%d" % h, align_bytes=64) for h in range(2)]
+
+        def quantize(h):
+            nc.vector.quantize_mx(
+                out=wa_codes[h][:].bitcast(FP8X4),
+                scales=wa_plane[h][:],
+                in_=wa_grouped[h][:].rearrange("p n t -> p (n t)"),
+            )
+
+        quantize(0)
+        quantize(1)
+        out_rows = out.rearrange("(b p) j -> p b j", p=P)
+        xt_codes = []
+        for s in range(2):
+            picked = sb.tile([P, HALF], U32, name="xt_codes%d" % s, align_bytes=64)
+            nc.vector.tensor_copy(picked[:], xt_table[:].indirect(xt_list[:, s * 16 : (s + 1) * 16]))
+            xt_codes.append(picked)
+
+        for s in range(2):
+            slots = slice(s * HALF, (s + 1) * HALF)
+            for h in range(2):
+                p_bank = psum.tile([P, 2, HALF], F32, name="p_bank%d%d" % (s, h))
+                for c in range(2):
+                    cols = slice(c * P, (c + 1) * P)
+                    nc.tensor.matmul_mx(
+                        out=p_bank[:, c, :],
+                        lhsT=wa_codes[h][:, cols].bitcast(FP8X4),
+                        lhsT_scale=wa_plane[h][:, cols],
+                        rhs=xt_codes[s][:].bitcast(FP8X4),
+                        rhs_scale=xt_plane[:, slots],
+                        start=True,
+                        stop=True,
+                    )
+                diff = sb.tile([P, 2, HALF], F32, name="diff%d%d" % (s, h))
+                nc.vector.tensor_tensor(diff[:], p_bank[:], q_scaled[:, 2 * h : 2 * h + 2, slots], ALU.add)
+                result = sb.tile([P, 2, HALF], F32, name="result%d%d" % (s, h))
+                if s == 1 and h == 1:
+                    nc.vector.tensor_scalar(result[:], diff[:], 0.0, None, ALU.max)
+                else:
+                    nc.scalar.activation(result[:], diff[:], ACT.Relu)
+                nc.sync.dma_start(out_rows[:, 2 * h : 2 * h + 2, slots], result[:])

@@ -34,43 +34,43 @@ def tile_moe_expert_heads_against_shared_kernel(
         xb_list = lists.tile([P, J // 16], U16, name="xb_list")
 
         xt_scale_table = sb.tile([P, T], U8, name="xt_scale_table", align_bytes=64)
-        xb_scale_table = sb.tile([P, T], U8, name="xb_scale_table", align_bytes=64)
+        xb_scale_table = sb.tile([P, T], U8, name="xb_scale_table", tag="reused", align_bytes=64)
         wb_plane = sb.tile([P, N], U8, name="wb_plane", align_bytes=64)
         xt_plane = sb.tile([P, J], U8, name="xt_plane", align_bytes=64)
+        nc.gpsimd.memset(xt_scale_table[:].bitcast(I32), 0)
+        nc.vector.memset(xb_scale_table[:].bitcast(I32), 0)
+        nc.vector.memset(wb_plane[:].bitcast(I32), 0)
         nc.vector.memset(xt_plane[:].bitcast(I32), 0)
 
         xt_table = sb.tile([P, T], U32, name="xt_table", align_bytes=64)
-        xb_table = sb.tile([P, T], U16, name="xb_table", tag="reused", align_bytes=64)
+        xb_table = sb.tile([P, T], U16, name="xb_table", align_bytes=64)
         wb_codes = sb.tile([P, N], U32, name="wb_codes", align_bytes=64)
         wa_raw = [sb.tile([P, 4, HALF], F32, name="wa_raw%d" % h, align_bytes=64) for h in range(2)]
         wa_rows = wa.rearrange("(p t) n -> p t n", t=4)
 
-        def load_rows(plane, scales):
-            for x in range(4):
-                rows = scales[0, 4 * x : 4 * x + 4, :].bitcast(I32)
-                nc.sync.dma_start(
-                    plane[32 * x : 32 * x + 32, :].bitcast(I32), rows.unsqueeze(0).to_broadcast([8, 4, rows.shape[1]])
-                )
+        def load_rows(queue, plane, scales, x):
+            queue.dma_start(plane[32 * x : 32 * x + 4, :].bitcast(I32), scales[0, 4 * x : 4 * x + 4, :].bitcast(I32))
 
-        nc.sync.dma_start(xt_list[:], offs)
-        nc.sync.dma_start(
-            xt_scale_table[:].bitcast(I32), xt_scales[0].bitcast(I32).unsqueeze(1).to_broadcast([16, 8, T // 4])
-        )
-        nc.sync.dma_start(wa_raw[0][:], wa_rows[:, :, 0:HALF])
         nc.sync.dma_start(xb_list[:], offs2)
-        load_rows(xb_scale_table, xb_scales)
         nc.sync.dma_start(xb_table[:].bitcast(I32), xb_words[0].bitcast(I32))
+        nc.sync.dma_start(xt_list[:], offs)
+        nc.sync.dma_start(xt_scale_table[0:P:8, :].bitcast(I32), xt_scales[0].bitcast(I32))
+        nc.sync.dma_start(wa_raw[0][:], wa_rows[:, :, 0:HALF])
+        for x in range(3):
+            load_rows(nc.sync, xb_scale_table, xb_scales, x)
         nc.sync.dma_start(wa_raw[1][:], wa_rows[:, :, HALF:N])
-        load_rows(wb_plane, wb_scales)
+        load_rows(nc.sync, xb_scale_table, xb_scales, 3)
         nc.sync.dma_start(wb_codes[:].bitcast(I32), wb_words[0].rearrange("p n t -> p (n t)").bitcast(I32))
+        for x in range(4):
+            load_rows(nc.sync, wb_plane, wb_scales, x)
         nc.sync.dma_start(xt_table[:].bitcast(I32), xt_words[0].rearrange("p n t -> p (n t)").bitcast(I32))
 
         xb_plane = sb.tile([P, J], U8, name="xb_plane", align_bytes=64)
         xb_codes = sb.tile([P, J], U16, name="xb_codes", align_bytes=64)
         xt_picked = sb.tile([P, J], U8, name="xt_picked", align_bytes=64)
+        nc.vector.tensor_copy(xb_codes[:], xb_table[:].indirect(xb_list[:]))
         nc.vector.tensor_copy(xt_picked[:], xt_scale_table[:].indirect(xt_list[:]))
         nc.vector.tensor_copy(xb_plane[:], xb_scale_table[:].indirect(xb_list[:]))
-        nc.vector.tensor_copy(xb_codes[:], xb_table[:].indirect(xb_list[:]))
         for x in range(4):
             nc.sync.dma_start(
                 xt_plane[32 * x : 32 * x + 4, :].bitcast(I32), xt_picked[32 * x : 32 * x + 32 : 8, :].bitcast(I32)
@@ -86,7 +86,7 @@ def tile_moe_expert_heads_against_shared_kernel(
 
         q_scaled = sb.tile([P, 4, J], F32, name="q_scaled")
         for b in range(4):
-            q_bank = psum.tile([P, J], F32, name="q_bank%d" % b)
+            q_bank = psum.tile([P, J], F32, name="q_bank%d" % b, tag="bank%d" % (4 + b))
             nc.tensor.matmul_mx(
                 out=q_bank[:],
                 lhsT=wb_codes[:, b * P : (b + 1) * P].bitcast(FP8X4),
@@ -98,48 +98,38 @@ def tile_moe_expert_heads_against_shared_kernel(
             )
             nc.scalar.activation(q_scaled[:, b, :], q_bank[:], ACT.Copy, scale=-0.7)
 
-        wa_codes = [
-            sb.tile([P, HALF], U32, name="wa_codes0", tag="reused", align_bytes=64),
-            sb.tile([P, HALF], U32, name="wa_codes1", align_bytes=64),
-        ]
-        wa_plane = [sb.tile([P, HALF], U8, name="wa_plane%d" % h, align_bytes=64) for h in range(2)]
-
-        def quantize(h):
+        wa_codes = sb.tile([P, N], U32, name="wa_codes", tag="reused", align_bytes=64)
+        wa_plane = sb.tile([P, N], U8, name="wa_plane", align_bytes=64)
+        for h in range(2):
+            cols = slice(h * HALF, (h + 1) * HALF)
             nc.vector.quantize_mx(
-                out=wa_codes[h][:].bitcast(FP8X4),
-                scales=wa_plane[h][:],
+                out=wa_codes[:, cols].bitcast(FP8X4),
+                scales=wa_plane[:, cols],
                 in_=wa_grouped[h][:].rearrange("p n t -> p (n t)"),
             )
 
-        quantize(0)
-        quantize(1)
-        out_rows = out.rearrange("(b p) j -> p b j", p=P)
         xt_codes = []
         for s in range(2):
             picked = sb.tile([P, HALF], U32, name="xt_codes%d" % s, align_bytes=64)
             nc.vector.tensor_copy(picked[:], xt_table[:].indirect(xt_list[:, s * 16 : (s + 1) * 16]))
             xt_codes.append(picked)
 
-        for s in range(2):
-            slots = slice(s * HALF, (s + 1) * HALF)
-            for h in range(2):
-                p_bank = psum.tile([P, 2, HALF], F32, name="p_bank%d%d" % (s, h))
-                for c in range(2):
-                    cols = slice(c * P, (c + 1) * P)
-                    nc.tensor.matmul_mx(
-                        out=p_bank[:, c, :],
-                        lhsT=wa_codes[h][:, cols].bitcast(FP8X4),
-                        lhsT_scale=wa_plane[h][:, cols],
-                        rhs=xt_codes[s][:].bitcast(FP8X4),
-                        rhs_scale=xt_plane[:, slots],
-                        start=True,
-                        stop=True,
-                    )
-                diff = sb.tile([P, 2, HALF], F32, name="diff%d%d" % (s, h))
-                nc.vector.tensor_tensor(diff[:], p_bank[:], q_scaled[:, 2 * h : 2 * h + 2, slots], ALU.add)
-                result = sb.tile([P, 2, HALF], F32, name="result%d%d" % (s, h))
-                if s == 1 and h == 1:
-                    nc.vector.tensor_scalar(result[:], diff[:], 0.0, None, ALU.max)
-                else:
-                    nc.scalar.activation(result[:], diff[:], ACT.Relu)
-                nc.sync.dma_start(out_rows[:, 2 * h : 2 * h + 2, slots], result[:])
+        for b in range(4):
+            rows = slice(b * P, (b + 1) * P)
+            for s in range(2):
+                slots = slice(s * HALF, (s + 1) * HALF)
+                p_bank = psum.tile([P, HALF], F32, name="p_bank%d%d" % (b, s), tag="bank%d" % (2 * b + s))
+                nc.tensor.matmul_mx(
+                    out=p_bank[:],
+                    lhsT=wa_codes[:, rows].bitcast(FP8X4),
+                    lhsT_scale=wa_plane[:, rows],
+                    rhs=xt_codes[s][:].bitcast(FP8X4),
+                    rhs_scale=xt_plane[:, slots],
+                    start=True,
+                    stop=True,
+                )
+                diff = sb.tile([P, HALF], F32, name="diff%d%d" % (b, s))
+                nc.vector.tensor_tensor(diff[:], p_bank[:], q_scaled[:, b, slots], ALU.add)
+                result = sb.tile([P, HALF], F32, name="result%d%d" % (b, s))
+                nc.scalar.activation(result[:], diff[:], ACT.Relu)
+                nc.sync.dma_start(out[rows, slots], result[:])

@@ -65,12 +65,15 @@ def tile_moe_expert_heads_against_shared_kernel(
             load_rows(nc.sync, wb_plane, wb_scales, x)
         nc.sync.dma_start(xt_table[:].bitcast(I32), xt_words[0].rearrange("p n t -> p (n t)").bitcast(I32))
 
-        xb_plane = sb.tile([P, J], U8, name="xb_plane", align_bytes=64)
         xb_codes = sb.tile([P, J], U16, name="xb_codes", align_bytes=64)
         xt_picked = sb.tile([P, J], U8, name="xt_picked", align_bytes=64)
         nc.vector.tensor_copy(xb_codes[:], xb_table[:].indirect(xb_list[:]))
         nc.vector.tensor_copy(xt_picked[:], xt_scale_table[:].indirect(xt_list[:]))
-        nc.vector.tensor_copy(xb_plane[:], xb_scale_table[:].indirect(xb_list[:]))
+        xb_plane = []
+        for s in range(2):
+            plane = sb.tile([P, HALF], U8, name="xb_plane%d" % s, align_bytes=64)
+            nc.vector.tensor_copy(plane[:], xb_scale_table[:].indirect(xb_list[:, s * 16 : (s + 1) * 16]))
+            xb_plane.append(plane)
         for x in range(4):
             nc.sync.dma_start(
                 xt_plane[32 * x : 32 * x + 4, :].bitcast(I32), xt_picked[32 * x : 32 * x + 32 : 8, :].bitcast(I32)
@@ -84,19 +87,21 @@ def tile_moe_expert_heads_against_shared_kernel(
             )
             wa_grouped.append(grouped)
 
-        q_scaled = sb.tile([P, 4, J], F32, name="q_scaled")
-        for b in range(4):
-            q_bank = psum.tile([P, J], F32, name="q_bank%d" % b, tag="bank%d" % (4 + b))
+        pieces = [(s, b) for s in range(2) for b in range(4)]
+        q_scaled = {}
+        for s, b in pieces:
+            q_bank = psum.tile([P, HALF], F32, name="q_bank%d%d" % (s, b), tag="bank%d%d" % (s, b))
             nc.tensor.matmul_mx(
                 out=q_bank[:],
                 lhsT=wb_codes[:, b * P : (b + 1) * P].bitcast(FP8X4),
                 lhsT_scale=wb_plane[:, b * P : (b + 1) * P],
-                rhs=xb_codes[:].bitcast(FP4X4),
-                rhs_scale=xb_plane[:],
+                rhs=xb_codes[:, s * HALF : (s + 1) * HALF].bitcast(FP4X4),
+                rhs_scale=xb_plane[s][:],
                 start=True,
                 stop=True,
             )
-            nc.scalar.activation(q_scaled[:, b, :], q_bank[:], ACT.Copy, scale=-0.7)
+            q_scaled[s, b] = sb.tile([P, HALF], F32, name="q_scaled%d%d" % (s, b))
+            nc.scalar.activation(q_scaled[s, b][:], q_bank[:], ACT.Copy, scale=-0.7)
 
         wa_codes = sb.tile([P, N], U32, name="wa_codes", tag="reused", align_bytes=64)
         wa_plane = sb.tile([P, N], U8, name="wa_plane", align_bytes=64)
@@ -114,22 +119,21 @@ def tile_moe_expert_heads_against_shared_kernel(
             nc.vector.tensor_copy(picked[:], xt_table[:].indirect(xt_list[:, s * 16 : (s + 1) * 16]))
             xt_codes.append(picked)
 
-        for b in range(4):
+        for s, b in pieces:
             rows = slice(b * P, (b + 1) * P)
-            for s in range(2):
-                slots = slice(s * HALF, (s + 1) * HALF)
-                p_bank = psum.tile([P, HALF], F32, name="p_bank%d%d" % (b, s), tag="bank%d" % (2 * b + s))
-                nc.tensor.matmul_mx(
-                    out=p_bank[:],
-                    lhsT=wa_codes[:, rows].bitcast(FP8X4),
-                    lhsT_scale=wa_plane[:, rows],
-                    rhs=xt_codes[s][:].bitcast(FP8X4),
-                    rhs_scale=xt_plane[:, slots],
-                    start=True,
-                    stop=True,
-                )
-                diff = sb.tile([P, HALF], F32, name="diff%d%d" % (b, s))
-                nc.vector.tensor_tensor(diff[:], p_bank[:], q_scaled[:, b, slots], ALU.add)
-                result = sb.tile([P, HALF], F32, name="result%d%d" % (b, s))
-                nc.scalar.activation(result[:], diff[:], ACT.Relu)
-                nc.sync.dma_start(out[rows, slots], result[:])
+            slots = slice(s * HALF, (s + 1) * HALF)
+            p_bank = psum.tile([P, HALF], F32, name="p_bank%d%d" % (s, b), tag="bank%d%d" % (s, b))
+            nc.tensor.matmul_mx(
+                out=p_bank[:],
+                lhsT=wa_codes[:, rows].bitcast(FP8X4),
+                lhsT_scale=wa_plane[:, rows],
+                rhs=xt_codes[s][:].bitcast(FP8X4),
+                rhs_scale=xt_plane[:, slots],
+                start=True,
+                stop=True,
+            )
+            diff = sb.tile([P, HALF], F32, name="diff%d%d" % (s, b))
+            nc.vector.tensor_tensor(diff[:], p_bank[:], q_scaled[s, b][:], ALU.add)
+            result = sb.tile([P, HALF], F32, name="result%d%d" % (s, b))
+            nc.scalar.activation(result[:], diff[:], ACT.Relu)
+            nc.sync.dma_start(out[rows, slots], result[:])

@@ -33,7 +33,7 @@ def tile_moe_expert_heads_against_shared_kernel(
         xt_list = lists.tile([P, J // 16], U16, name="xt_list")
         xb_list = lists.tile([P, J // 16], U16, name="xb_list")
 
-        xt_scale_table = sb.tile([P, T], U8, name="xt_scale_table", align_bytes=64)
+        xt_scale_table = sb.tile([P, T], U8, name="xt_scale_table", tag="first", align_bytes=64)
         xb_scale_table = sb.tile([P, T], U8, name="xb_scale_table", tag="reused", align_bytes=64)
         wb_plane = sb.tile([P, N], U8, name="wb_plane", align_bytes=64)
         xt_plane = sb.tile([P, J], U8, name="xt_plane", align_bytes=64)
@@ -45,7 +45,8 @@ def tile_moe_expert_heads_against_shared_kernel(
         xt_table = sb.tile([P, T], U32, name="xt_table", align_bytes=64)
         xb_table = sb.tile([P, T], U16, name="xb_table", align_bytes=64)
         wb_codes = sb.tile([P, N], U32, name="wb_codes", align_bytes=64)
-        wa_raw = [sb.tile([P, 4, HALF], F32, name="wa_raw%d" % h, align_bytes=64) for h in range(2)]
+        wa_early = sb.tile([P, 4, 3 * P], F32, name="wa_early", align_bytes=64)
+        wa_late = sb.tile([P, 4, P], F32, name="wa_late", align_bytes=64)
         wa_rows = wa.rearrange("(p t) n -> p t n", t=4)
 
         def load_rows(queue, plane, scales, x):
@@ -55,20 +56,20 @@ def tile_moe_expert_heads_against_shared_kernel(
         nc.sync.dma_start(xb_table[:].bitcast(I32), xb_words[0].bitcast(I32))
         nc.sync.dma_start(xt_list[:], offs)
         nc.sync.dma_start(xt_scale_table[0:P:8, :].bitcast(I32), xt_scales[0].bitcast(I32))
-        nc.sync.dma_start(wa_raw[0][:], wa_rows[:, :, 0:HALF])
         for x in range(3):
             load_rows(nc.sync, xb_scale_table, xb_scales, x)
-        nc.sync.dma_start(wa_raw[1][:], wa_rows[:, :, HALF:N])
+        nc.sync.dma_start(wa_early[:], wa_rows[:, :, 0 : 3 * P])
         load_rows(nc.sync, xb_scale_table, xb_scales, 3)
         nc.sync.dma_start(wb_codes[:].bitcast(I32), wb_words[0].rearrange("p n t -> p (n t)").bitcast(I32))
         for x in range(4):
             load_rows(nc.sync, wb_plane, wb_scales, x)
         nc.sync.dma_start(xt_table[:].bitcast(I32), xt_words[0].rearrange("p n t -> p (n t)").bitcast(I32))
+        nc.sync.dma_start(wa_late[:], wa_rows[:, :, 3 * P : N])
 
-        xb_codes = sb.tile([P, J], U16, name="xb_codes", align_bytes=64)
+        xb_codes = sb.tile([P, J], U16, name="xb_codes", tag="first", align_bytes=64)
         xt_picked = sb.tile([P, J], U8, name="xt_picked", align_bytes=64)
-        nc.vector.tensor_copy(xb_codes[:], xb_table[:].indirect(xb_list[:]))
         nc.vector.tensor_copy(xt_picked[:], xt_scale_table[:].indirect(xt_list[:]))
+        nc.vector.tensor_copy(xb_codes[:], xb_table[:].indirect(xb_list[:]))
         xb_plane = []
         for s in range(2):
             plane = sb.tile([P, HALF], U8, name="xb_plane%d" % s, align_bytes=64)
@@ -80,12 +81,15 @@ def tile_moe_expert_heads_against_shared_kernel(
             )
 
         wa_grouped = []
-        for h in range(2):
-            grouped = sb.tile([P, HALF, 4], BF16, name="wa_grouped%d" % h, align_bytes=64)
-            nc.scalar.copy(
-                grouped[:].rearrange("p (c i) t -> p c t i", i=4), wa_raw[h][:].rearrange("p t (c i) -> p c t i", i=4)
-            )
-            wa_grouped.append(grouped)
+        for copy, raw, start in (
+            (nc.scalar.copy, wa_early[:, :, 0 : 2 * P], 0),
+            (nc.scalar.copy, wa_early[:, :, 2 * P : 3 * P], 2 * P),
+            (nc.vector.tensor_copy, wa_late[:], 3 * P),
+        ):
+            width = raw.shape[2]
+            grouped = sb.tile([P, width, 4], BF16, name="wa_grouped%d" % start, align_bytes=64)
+            copy(grouped[:].rearrange("p (c i) t -> p c t i", i=4), raw.rearrange("p t (c i) -> p c t i", i=4))
+            wa_grouped.append((grouped, slice(start, start + width)))
 
         pieces = [(s, b) for s in range(2) for b in range(4)]
         q_scaled = {}
@@ -103,15 +107,17 @@ def tile_moe_expert_heads_against_shared_kernel(
             q_scaled[s, b] = sb.tile([P, HALF], F32, name="q_scaled%d%d" % (s, b))
             nc.scalar.activation(q_scaled[s, b][:], q_bank[:], ACT.Copy, scale=-0.7)
 
-        wa_codes = sb.tile([P, N], U32, name="wa_codes", tag="reused", align_bytes=64)
-        wa_plane = sb.tile([P, N], U8, name="wa_plane", align_bytes=64)
-        for h in range(2):
-            cols = slice(h * HALF, (h + 1) * HALF)
+        wa_block = []
+        for grouped, cols in wa_grouped:
+            width = cols.stop - cols.start
+            tag = "reused" if cols.start == 0 else "wa_codes%d" % cols.start
+            codes = sb.tile([P, width], U32, name="wa_codes%d" % cols.start, tag=tag, align_bytes=64)
+            plane = sb.tile([P, width], U8, name="wa_plane%d" % cols.start, align_bytes=64)
             nc.vector.quantize_mx(
-                out=wa_codes[:, cols].bitcast(FP8X4),
-                scales=wa_plane[:, cols],
-                in_=wa_grouped[h][:].rearrange("p n t -> p (n t)"),
+                out=codes[:].bitcast(FP8X4), scales=plane[:], in_=grouped[:].rearrange("p n t -> p (n t)")
             )
+            for first in range(0, width, P):
+                wa_block.append((codes[:, first : first + P], plane[:, first : first + P]))
 
         xt_codes = []
         for s in range(2):
@@ -125,8 +131,8 @@ def tile_moe_expert_heads_against_shared_kernel(
             p_bank = psum.tile([P, HALF], F32, name="p_bank%d%d" % (s, b), tag="bank%d%d" % (s, b))
             nc.tensor.matmul_mx(
                 out=p_bank[:],
-                lhsT=wa_codes[:, rows].bitcast(FP8X4),
-                lhsT_scale=wa_plane[:, rows],
+                lhsT=wa_block[b][0].bitcast(FP8X4),
+                lhsT_scale=wa_block[b][1],
                 rhs=xt_codes[s][:].bitcast(FP8X4),
                 rhs_scale=xt_plane[:, slots],
                 start=True,

from contextlib import ExitStack

import concourse.mybir as mybir

F32 = mybir.dt.float32
BF16 = mybir.dt.bfloat16
I32 = mybir.dt.int32
U32 = mybir.dt.uint32
U16 = mybir.dt.uint16
U8 = mybir.dt.uint8
FP8X4 = mybir.dt.float8_e4m3fn_x4
FP4X4 = mybir.dt.float4_e2m1fn_x4
ALU = mybir.AluOpType
ACT = mybir.ActivationFunctionType

P = 128
T = 1024
J = 512
N = 512
HALF = N // 2
FLOPS = 2 * 2 * 512 * N * J


def tile_moe_expert_heads_against_shared_kernel(
    tc, xt_words, xt_scales, wa, xb_words, xb_scales, wb_words, wb_scales, offs, offs2, out
):
    nc = tc.nc
    with ExitStack() as ctx:
        lists = ctx.enter_context(tc.tile_pool(name="lists", bufs=1))
        sb = ctx.enter_context(tc.tile_pool(name="sb", bufs=1))
        psum = ctx.enter_context(tc.psum_pool(name="psum", bufs=1))

        xt_list = lists.tile([P, J // 16], U16, name="xt_list")
        xb_list = lists.tile([P, J // 16], U16, name="xb_list")

        xt_scale_table = sb.tile([P, T], U8, name="xt_scale_table", tag="first", align_bytes=64)
        xb_scale_table = sb.tile([P, T], U8, name="xb_scale_table", tag="reused", align_bytes=64)
        wb_plane = sb.tile([P, N], U8, name="wb_plane", align_bytes=64)
        xt_plane = sb.tile([P, J], U8, name="xt_plane", align_bytes=64)
        nc.gpsimd.memset(xt_scale_table[:].bitcast(I32), 0)
        nc.vector.memset(xb_scale_table[:].bitcast(I32), 0)
        nc.vector.memset(wb_plane[:].bitcast(I32), 0)
        nc.vector.memset(xt_plane[:].bitcast(I32), 0)

        xt_table = sb.tile([P, T], U32, name="xt_table", align_bytes=64)
        xb_table = sb.tile([P, T], U16, name="xb_table", align_bytes=64)
        wb_codes = sb.tile([P, N], U32, name="wb_codes", align_bytes=64)
        wa_early = sb.tile([P, 4, 3 * P], F32, name="wa_early", align_bytes=64)
        wa_late = sb.tile([P, 4, P], F32, name="wa_late", align_bytes=64)
        wa_rows = wa.rearrange("(p t) n -> p t n", t=4)

        def load_rows(queue, plane, scales, x):
            queue.dma_start(plane[32 * x : 32 * x + 4, :].bitcast(I32), scales[0, 4 * x : 4 * x + 4, :].bitcast(I32))

        nc.sync.dma_start(xb_list[:], offs2)
        nc.sync.dma_start(xb_table[:].bitcast(I32), xb_words[0].bitcast(I32))
        nc.sync.dma_start(xt_list[:], offs)
        nc.sync.dma_start(xt_scale_table[0:P:8, :].bitcast(I32), xt_scales[0].bitcast(I32))
        for x in range(3):
            load_rows(nc.sync, xb_scale_table, xb_scales, x)
        nc.sync.dma_start(wa_early[:], wa_rows[:, :, 0 : 3 * P])
        load_rows(nc.sync, xb_scale_table, xb_scales, 3)
        nc.sync.dma_start(wb_codes[:].bitcast(I32), wb_words[0].rearrange("p n t -> p (n t)").bitcast(I32))
        for x in range(4):
            load_rows(nc.sync, wb_plane, wb_scales, x)
        nc.sync.dma_start(xt_table[:].bitcast(I32), xt_words[0].rearrange("p n t -> p (n t)").bitcast(I32))
        nc.sync.dma_start(wa_late[:], wa_rows[:, :, 3 * P : N])

        xb_codes = sb.tile([P, J], U16, name="xb_codes", tag="first", align_bytes=64)
        xt_picked = sb.tile([P, J], U8, name="xt_picked", align_bytes=64)
        nc.vector.tensor_copy(xt_picked[:], xt_scale_table[:].indirect(xt_list[:]))
        nc.vector.tensor_copy(xb_codes[:], xb_table[:].indirect(xb_list[:]))
        xb_plane = []
        for s in range(2):
            plane = sb.tile([P, HALF], U8, name="xb_plane%d" % s, align_bytes=64)
            nc.vector.tensor_copy(plane[:], xb_scale_table[:].indirect(xb_list[:, s * 16 : (s + 1) * 16]))
            xb_plane.append(plane)
        for x in range(4):
            nc.sync.dma_start(
                xt_plane[32 * x : 32 * x + 4, :].bitcast(I32), xt_picked[32 * x : 32 * x + 32 : 8, :].bitcast(I32)
            )

        wa_grouped = []
        for copy, raw, start in (
            (nc.scalar.copy, wa_early[:, :, 0 : 2 * P], 0),
            (nc.scalar.copy, wa_early[:, :, 2 * P : 3 * P], 2 * P),
            (nc.vector.tensor_copy, wa_late[:], 3 * P),
        ):
            width = raw.shape[2]
            grouped = sb.tile([P, width, 4], BF16, name="wa_grouped%d" % start, align_bytes=64)
            copy(grouped[:].rearrange("p (c i) t -> p c t i", i=4), raw.rearrange("p t (c i) -> p c t i", i=4))
            wa_grouped.append((grouped, slice(start, start + width)))

        pieces = [(s, b) for s in range(2) for b in range(4)]
        q_scaled = {}
        for s, b in pieces:
            q_bank = psum.tile([P, HALF], F32, name="q_bank%d%d" % (s, b), tag="bank%d%d" % (s, b))
            nc.tensor.matmul_mx(
                out=q_bank[:],
                lhsT=wb_codes[:, b * P : (b + 1) * P].bitcast(FP8X4),
                lhsT_scale=wb_plane[:, b * P : (b + 1) * P],
                rhs=xb_codes[:, s * HALF : (s + 1) * HALF].bitcast(FP4X4),
                rhs_scale=xb_plane[s][:],
                start=True,
                stop=True,
            )
            q_scaled[s, b] = sb.tile([P, HALF], F32, name="q_scaled%d%d" % (s, b))
            nc.scalar.activation(q_scaled[s, b][:], q_bank[:], ACT.Copy, scale=-0.7)

        wa_block = []
        for grouped, cols in wa_grouped:
            width = cols.stop - cols.start
            tag = "reused" if cols.start == 0 else "wa_codes%d" % cols.start
            codes = sb.tile([P, width], U32, name="wa_codes%d" % cols.start, tag=tag, align_bytes=64)
            plane = sb.tile([P, width], U8, name="wa_plane%d" % cols.start, align_bytes=64)
            nc.vector.quantize_mx(
                out=codes[:].bitcast(FP8X4), scales=plane[:], in_=grouped[:].rearrange("p n t -> p (n t)")
            )
            for first in range(0, width, P):
                wa_block.append((codes[:, first : first + P], plane[:, first : first + P]))

        xt_codes = []
        for s in range(2):
            picked = sb.tile([P, HALF], U32, name="xt_codes%d" % s, align_bytes=64)
            nc.vector.tensor_copy(picked[:], xt_table[:].indirect(xt_list[:, s * 16 : (s + 1) * 16]))
            xt_codes.append(picked)

        for s, b in pieces:
            rows = slice(b * P, (b + 1) * P)
            slots = slice(s * HALF, (s + 1) * HALF)
            p_bank = psum.tile([P, HALF], F32, name="p_bank%d%d" % (s, b), tag="bank%d%d" % (s, b))
            nc.tensor.matmul_mx(
                out=p_bank[:],
                lhsT=wa_block[b][0].bitcast(FP8X4),
                lhsT_scale=wa_block[b][1],
                rhs=xt_codes[s][:].bitcast(FP8X4),
                rhs_scale=xt_plane[:, slots],
                start=True,
                stop=True,
            )
            diff = sb.tile([P, HALF], F32, name="diff%d%d" % (s, b))
            nc.vector.tensor_tensor(diff[:], p_bank[:], q_scaled[s, b][:], ALU.add)
            result = sb.tile([P, HALF], F32, name="result%d%d" % (s, b))
            nc.scalar.activation(result[:], diff[:], ACT.Relu)
            nc.sync.dma_start(out[rows, slots], result[:])
